import numpy as np
import ml_dtypes


def mxq(x, axis, fmt="e4m3"):
    dtype, down = {"e4m3": (ml_dtypes.float8_e4m3fn, 7), "e5m2": (ml_dtypes.float8_e5m2, 14)}[fmt]
    v = np.moveaxis(np.asarray(x, np.float32).astype(ml_dtypes.bfloat16).astype(np.float64), axis, -1)
    blocks = v.reshape(v.shape[:-1] + (-1, 32))
    amax = np.abs(blocks).max(-1, keepdims=True)
    byte = np.maximum(np.where(amax > 0, np.frexp(amax)[1] - 1 + 127, 0) - down, 1)
    scale = np.exp2(byte - 127.0)
    codes = (blocks / scale).astype(np.float32).astype(dtype).astype(np.float64)
    return np.moveaxis((codes * scale).reshape(v.shape), -1, axis)


WIDE = False


def mx_kscale(k):
    if not WIDE:
        return np.ones(k)
    levels = np.array([10, -10, 5, -5, 0])
    if k % 512:
        return np.exp2(np.random.permutation(np.resize(levels, k // 32))).repeat(32)
    a = np.empty((k // 512, 16))
    for p in range(k // 512):
        a[p, :8] = np.random.permutation(np.resize(levels, 8))
        for g in range(8):
            far = levels[np.abs(levels - a[p, g]) >= 10]
            a[p, g + 8] = far[np.random.randint(len(far))]
    return np.exp2(a.ravel()).repeat(32)


def f64(x):
    return np.asarray(x).astype(np.float64)


def striped(idx):
    return np.tile(idx.reshape(-1, 16).T, (8, 1)).astype(np.uint16)


def unstriped(offs):
    return offs[:16].T.reshape(-1).astype(np.int64)


def striped8(idx):
    return np.concatenate([x.reshape(-1, 16).T for x in idx]).astype(np.uint16)


def runs(offs, k):
    lists = np.stack([offs[16 * r : 16 * r + 16].T.reshape(-1) for r in range(8)]).astype(np.int64)
    return lists[np.arange(k) % 512 // 64]


def pack_weight(w):
    k, n = w.shape
    w = f64(np.asarray(w, np.float32).astype(ml_dtypes.bfloat16)).reshape(k // 32, 32, n)
    amax = np.abs(w).max(1)
    byte = np.clip(np.where(amax > 0, np.frexp(amax)[1] - 1 + 127 - 7, 1), 1, 254)
    scaled = (w * np.exp2(127.0 - byte)[:, None, :]).reshape(k, n).astype(np.float32)
    words = np.ascontiguousarray(scaled.reshape(k // 512, 128, 4, n).transpose(0, 1, 3, 2)).astype(ml_dtypes.float8_e4m3fn).view(np.uint8)
    return words, np.ascontiguousarray(byte.astype(np.uint8).reshape(k // 512, 16, n))


def unpack_weight(words, scales):
    g, p, n, _ = words.shape
    vals = np.ascontiguousarray(words).view(ml_dtypes.float8_e4m3fn).astype(np.float64) * np.repeat(np.exp2(scales.astype(np.float64) - 127.0), 8, axis=1)[..., None]
    return vals.transpose(0, 1, 3, 2).reshape(g * 512, n)


def relu(v):
    return np.maximum(v, 0.0)

def planes(y):
    n, m = y.shape
    v = y.astype(np.float32).astype(ml_dtypes.bfloat16).astype(np.float64).reshape(n // 32, 32, m)
    top = np.abs(v).max(1)
    byte = np.clip(np.where(top > 0, np.frexp(top)[1] - 1 + 127 - 7, 1), 1, 254)
    codes = (v * np.exp2(127.0 - byte)[:, None, :]).reshape(n, m).astype(np.float32).astype(ml_dtypes.float8_e4m3fn).view(np.uint8)
    words = codes.reshape(n // 512, 128, 4, m).transpose(0, 1, 3, 2)
    return np.ascontiguousarray(words), np.ascontiguousarray(byte.astype(np.uint8).reshape(n // 512, 16, m))


K, T, S, G, H = 512, 2048, 512, 2048, 512


def setup_inputs():
    n = np.random.standard_normal
    s = mx_kscale(K)[:, None]
    packed_xT = pack_weight(n((K, T)) * s)
    packed_dT = pack_weight(n((K, G)) / s)
    return {
        "x_words": packed_xT[0],
        "x_scales": packed_xT[1],
        "d_words": packed_dT[0],
        "d_scales": packed_dT[1],
        "gs": (np.random.uniform(0.5, 1.5, (K, 1)) * s).astype(np.float32),
        "offs": striped(np.random.permutation(T)[:S]),
        "k1": striped8(np.random.randint(0, G, (8, H))),
        "k2": striped8(np.random.randint(0, G, (8, H))),
        "k3": striped8(np.random.randint(0, G, (8, H))),
        "k4": striped8(np.random.randint(0, G, (8, H))),
    }


def reference(x_words, x_scales, d_words, d_scales, gs, offs, k1, k2, k3, k4):
    d_k3 = unpack_weight(d_words, d_scales)[np.arange(K)[:, None], runs(k3, K)]
    d_k1 = unpack_weight(d_words, d_scales)[np.arange(K)[:, None], runs(k1, K)]
    xq = unpack_weight(x_words, x_scales)[:, unstriped(offs)]
    d_k2 = unpack_weight(d_words, d_scales)[np.arange(K)[:, None], runs(k2, K)]
    h = relu(0.0625 * ((d_k1.T @ xq) + 0.25 * (d_k2.T @ xq)))
    z = f64(gs) * h
    zq = mxq(z, 0, "e4m3")
    d_k4 = unpack_weight(d_words, d_scales)[np.arange(K)[:, None], runs(k4, K)]
    out_0 = 0.0625 * ((d_k3.T @ zq) + 0.25 * (d_k4.T @ zq))
    return (out_0,) + planes(out_0)

@@ -1,0 +1,195 @@
+from contextlib import ExitStack
+
+import concourse.mybir as mybir
+from concourse.masks import make_identity
+
+K, T, S, G, H = 512, 2048, 512, 2048, 512
+FLOPS = 4 * 2 * K * H * S
+
+F32 = mybir.dt.float32
+BF16 = mybir.dt.bfloat16
+I32 = mybir.dt.int32
+U32 = mybir.dt.uint32
+U16 = mybir.dt.uint16
+U8 = mybir.dt.uint8
+FP8X4 = mybir.dt.float8_e4m3fn_x4
+ALU = mybir.AluOpType
+ACT = mybir.ActivationFunctionType
+
+P = 128
+PACK = 4
+CH = 128
+NCH = S // CH
+COARSE = 0.0625
+FINE = 0.0625 * 0.25
+
+
+def tile_picked_pqres2_relu_po_kernel(
+    tc, x_words, x_scales, d_words, d_scales, gs, offs, k1, k2, k3, k4, out_0, out_1, out_2
+):
+    nc = tc.nc
+    with ExitStack() as ctx:
+        lists = ctx.enter_context(tc.tile_pool(name="lists", bufs=1))
+        keep = ctx.enter_context(tc.tile_pool(name="keep", bufs=1))
+        shared = ctx.enter_context(tc.tile_pool(name="shared", bufs=1))
+        psum = ctx.enter_context(tc.psum_pool(name="psum", bufs=8))
+
+        def list_tile(name):
+            return lists.tile([P, S // 16], U16, name=name)
+
+        k1_sb, k2_sb, k3_sb, k4_sb, offs_sb = [list_tile(n) for n in ("k1_sb", "k2_sb", "k3_sb", "k4_sb", "offs_sb")]
+
+        d_byte_win = keep.tile([P, G], U8, align_bytes=64)
+        x_byte_win = keep.tile([P, T], U8, align_bytes=64)
+        d_word_win = keep.tile([P, G], U32, align_bytes=64)
+        x_word_win = shared.tile([P, T], U32, align_bytes=64, offset=0)
+        planes1 = keep.tile([P, 3, S], U8, align_bytes=64)
+        planes2 = keep.tile([P, H], U8, align_bytes=64)
+        gs_sb = keep.tile([P, 1, PACK], F32)
+        ident = keep.tile([P, P], F32, align_bytes=64)
+
+        nc.vector.memset(d_byte_win[:].bitcast(I32), 0)
+        nc.vector.memset(x_byte_win[:].bitcast(I32), 0)
+
+        nc.sync.dma_start(k1_sb[:], k1)
+        nc.sync.dma_start(d_byte_win[:].bitcast(I32)[0:P:8, :], d_scales[0].bitcast(I32))
+        nc.sync.dma_start(offs_sb[:], offs)
+        nc.sync.dma_start(x_byte_win[:].bitcast(I32)[0:P:8, :], x_scales[0].bitcast(I32))
+        nc.sync.dma_start(k2_sb[:], k2)
+        nc.sync.dma_start(k3_sb[:], k3)
+        nc.sync.dma_start(k4_sb[:], k4)
+        nc.sync.dma_start(d_word_win[:].bitcast(I32), d_words[0].rearrange("p n t -> p (n t)").bitcast(I32))
+        nc.sync.dma_start(x_word_win[:].bitcast(I32), x_words[0].rearrange("p n t -> p (n t)").bitcast(I32))
+        nc.sync.dma_start(gs_sb[:, 0, :], gs.rearrange("(p t) o -> p (t o)", t=PACK))
+
+        nc.vector.memset(planes1[:].rearrange("p l n -> p (l n)").bitcast(I32), 0)
+        nc.vector.memset(planes2[:].bitcast(I32), 0)
+        make_identity(nc, ident[:])
+
+        def place_rows(planes, first_row, picked):
+            for a in range(4):
+                nc.sync.dma_start(planes.bitcast(I32)[first_row + a : P : 32, :], picked.bitcast(I32)[8 * a : P : 32, :])
+
+        bytes1 = keep.tile([P, 3, S], U8, align_bytes=64)
+        nc.vector.tensor_copy(bytes1[:, 0, :], d_byte_win[:].indirect(k1_sb[:]))
+        nc.vector.tensor_copy(bytes1[:, 1, :], x_byte_win[:].indirect(offs_sb[:]))
+        nc.vector.tensor_copy(bytes1[:, 2, :], d_byte_win[:].indirect(k2_sb[:]))
+        place_rows(planes1[:].rearrange("p l n -> p (l n)"), 0, bytes1[:].rearrange("p l n -> p (l n)"))
+
+        d1_words = keep.tile([P, H], U32, align_bytes=64)
+        d2_words = keep.tile([P, H], U32, align_bytes=64)
+        nc.vector.tensor_copy(d1_words[:], d_word_win[:].indirect(k1_sb[:]))
+        nc.vector.tensor_copy(d2_words[:], d_word_win[:].indirect(k2_sb[:]))
+        xq = []
+        for h in range(2):
+            half = keep.tile([P, S // 2], U32, align_bytes=64, name="xq%d" % h)
+            nc.vector.tensor_copy(half[:], x_word_win[:].indirect(offs_sb[:, 16 * h : 16 * (h + 1)]))
+            xq.append(half)
+
+        bytes2 = shared.tile([P, 2, H], U8, align_bytes=64, offset=0)
+        words2 = shared.tile([P, 2, H], U32, align_bytes=64, offset=2048)
+        nc.vector.tensor_copy(bytes2[:, 0, :], d_byte_win[:].indirect(k3_sb[:]))
+        place_rows(planes2[:], 0, bytes2[:, 0, :])
+        nc.vector.tensor_copy(bytes2[:, 1, :], d_byte_win[:].indirect(k4_sb[:]))
+        place_rows(planes2[:], 4, bytes2[:, 1, :])
+        nc.vector.tensor_copy(words2[:, 0, :], d_word_win[:].indirect(k3_sb[:]))
+        nc.vector.tensor_copy(words2[:, 1, :], d_word_win[:].indirect(k4_sb[:]))
+        w2 = keep.tile([P, 2, PACK, P], U32, align_bytes=64)
+        s2 = keep.tile([P, PACK, P], U8, align_bytes=64)
+        nc.vector.tensor_copy(w2[:].bitcast(I32).rearrange("p l t m -> p l m t"), words2[:].bitcast(I32).rearrange("p l (m t) -> p l m t", t=PACK))
+        nc.vector.tensor_copy(s2[:].rearrange("p t m -> p m t"), planes2[:].rearrange("p (m t) -> p m t", t=PACK))
+
+        def first_products(c):
+            tok = slice(c * CH, (c + 1) * CH)
+            x_c = xq[c // 2][:, (c % 2) * CH : (c % 2 + 1) * CH]
+            parts = []
+            for words, plane, factor in ((d1_words, 0, COARSE), (d2_words, 2, FINE)):
+                acc = psum.tile([P, H], F32, tag="acc", name="acc")
+                nc.tensor.matmul_mx(
+                    out=acc[:], lhsT=x_c.bitcast(FP8X4), lhsT_scale=planes1[:, 1, tok],
+                    rhs=words[:].bitcast(FP8X4), rhs_scale=planes1[:, plane, :], start=True, stop=True,
+                )
+                part = keep.tile([P, PACK, P], F32, align_bytes=64, name="part%d_%d" % (c, plane))
+                nc.scalar.activation(part[:], acc[:].rearrange("p (m t) -> p t m", t=PACK), ACT.Copy, scale=factor)
+                parts.append(part)
+            return parts
+
+        def turn_and_add(parts):
+            u = psum.tile([P, PACK, CH], F32, tag="acc", name="u")
+            for t in range(PACK):
+                for i, part in enumerate(parts):
+                    nc.tensor.matmul(u[:, t, :], lhsT=part[:, t, :], rhs=ident[:], is_transpose=True, start=(i == 0), stop=(i == 1))
+            return u
+
+        pre = []
+        parts = first_products(0)
+        for c in range(NCH):
+            nxt = first_products(c + 1) if c + 1 < NCH else None
+            pre.append(turn_and_add(parts))
+            parts = nxt
+
+        y_view = out_0.rearrange("(p t) n -> p t n", t=PACK)
+        word_view = out_1[0].rearrange("p n t -> p (n t)").bitcast(I32)
+        y_scales = keep.tile([P, S], U8, align_bytes=64)
+
+        def hidden(c):
+            z = keep.tile([P, CH, PACK], BF16, align_bytes=64, name="z%d" % c)
+            nc.vector.scalar_tensor_tensor(
+                z[:], pre[c][:].rearrange("p t n -> p n t"), 0.0, gs_sb[:].to_broadcast([P, CH, PACK]), ALU.max, ALU.mult
+            )
+            return z
+
+        def second_products(c, z):
+            z_words = keep.tile([P, CH], U32, align_bytes=64, name="zw%d" % c)
+            z_scales = keep.tile([P, CH], U8, align_bytes=64, name="zs%d" % c)
+            nc.vector.quantize_mx(out=z_words[:].bitcast(FP8X4), scales=z_scales[:], in_=z[:].rearrange("p n t -> p (n t)"))
+            accs = []
+            for l in (1, 0):
+                acc = psum.tile([P, PACK, CH], F32, tag="acc", name="acc")
+                for t in range(PACK):
+                    nc.tensor.matmul_mx(
+                        out=acc[:, t, :], lhsT=w2[:, l, t, :].bitcast(FP8X4), lhsT_scale=s2[4 * l : P, t, :],
+                        rhs=z_words[:].bitcast(FP8X4), rhs_scale=z_scales[:], start=True, stop=True,
+                    )
+                accs.append(acc)
+            fine = keep.tile([P, PACK * CH], F32, align_bytes=64, name="fine%d" % c)
+            nc.scalar.activation(fine[:], accs[0][:].rearrange("p t n -> p (t n)"), ACT.Copy, scale=FINE)
+            return accs[1], fine
+
+        def combine(c, acc, fine):
+            tok = slice(c * CH, (c + 1) * CH)
+            y = keep.tile([P, PACK, CH], F32, align_bytes=64, name="y%d" % c)
+            nc.vector.scalar_tensor_tensor(
+                y[:].rearrange("p t n -> p (t n)"), acc[:].rearrange("p t n -> p (t n)"), COARSE, fine[:], ALU.mult, ALU.add
+            )
+            nc.sync.dma_start(y_view[:, :, tok], y[:])
+            y16 = keep.tile([P, CH, PACK], BF16, align_bytes=64, name="y16_%d" % c)
+            if c + 1 < NCH:
+                nc.scalar.copy(y16[:], y[:].rearrange("p t n -> p n t"))
+            else:
+                nc.vector.tensor_copy(y16[:], y[:].rearrange("p t n -> p n t"))
+            return y16
+
+        def hand_on(c, y16):
+            tok = slice(c * CH, (c + 1) * CH)
+            y_words = keep.tile([P, CH], U32, align_bytes=64, name="yw%d" % c)
+            nc.vector.quantize_mx(out=y_words[:].bitcast(FP8X4), scales=y_scales[:, tok], in_=y16[:].rearrange("p n t -> p (n t)"))
+            nc.sync.dma_start(word_view[:, tok], y_words[:].bitcast(I32))
+
+        zs = {}
+        prods = {}
+        y16s = {}
+        for step in range(NCH + 3):
+            if step < NCH:
+                zs[step] = hidden(step)
+            if 0 <= step - 2 < NCH:
+                y16s[step - 2] = combine(step - 2, *prods[step - 2])
+            if 0 <= step - 3 < NCH:
+                hand_on(step - 3, y16s[step - 3])
+            if 0 <= step - 1 < NCH:
+                prods[step - 1] = second_products(step - 1, zs[step - 1])
+
+        scale_view = out_2[0].bitcast(I32)
+        for a in range(4):
+            eng = nc.sync if a % 2 == 0 else nc.scalar
+            eng.dma_start(scale_view[a:16:4, :], y_scales[:].bitcast(I32)[a:P:32, :])

@@ -40,12 +40,11 @@ def tile_picked_pqres2_relu_po_kernel(
         k1_sb, k2_sb, k3_sb, k4_sb, offs_sb = [list_tile(n) for n in ("k1_sb", "k2_sb", "k3_sb", "k4_sb", "offs_sb")]
 
         d_byte_win = keep.tile([P, G], U8, align_bytes=64)
-        x_byte_win = keep.tile([P, T], U8, align_bytes=64)
+        x_byte_win = shared.tile([P, T], U8, align_bytes=64, offset=12288)
         d_word_win = keep.tile([P, G], U32, align_bytes=64)
         x_word_win = shared.tile([P, T], U32, align_bytes=64, offset=0)
         planes1 = keep.tile([P, 3, S], U8, align_bytes=64)
-        planes2 = keep.tile([P, H], U8, align_bytes=64)
-        gs_sb = keep.tile([P, 1, PACK], F32)
+        planes2 = shared.tile([P, H], U8, align_bytes=64, offset=10240)
         ident = keep.tile([P, P], F32, align_bytes=64)
 
         nc.vector.memset(d_byte_win[:].bitcast(I32), 0)
@@ -60,21 +59,24 @@ def tile_picked_pqres2_relu_po_kernel(
         nc.sync.dma_start(k4_sb[:], k4)
         nc.sync.dma_start(d_word_win[:].bitcast(I32), d_words[0].rearrange("p n t -> p (n t)").bitcast(I32))
         nc.sync.dma_start(x_word_win[:].bitcast(I32), x_words[0].rearrange("p n t -> p (n t)").bitcast(I32))
-        nc.sync.dma_start(gs_sb[:, 0, :], gs.rearrange("(p t) o -> p (t o)", t=PACK))
 
         nc.vector.memset(planes1[:].rearrange("p l n -> p (l n)").bitcast(I32), 0)
         nc.vector.memset(planes2[:].bitcast(I32), 0)
         make_identity(nc, ident[:])
 
         def place_rows(planes, first_row, picked):
-            for a in range(4):
-                nc.sync.dma_start(planes.bitcast(I32)[first_row + a : P : 32, :], picked.bitcast(I32)[8 * a : P : 32, :])
+            for q in range(4):
+                row = 32 * q + first_row
+                nc.sync.dma_start(planes.bitcast(I32)[row : row + 4, :], picked.bitcast(I32)[32 * q : 32 * q + 32 : 8, :])
 
         bytes1 = keep.tile([P, 3, S], U8, align_bytes=64)
         nc.vector.tensor_copy(bytes1[:, 0, :], d_byte_win[:].indirect(k1_sb[:]))
-        nc.vector.tensor_copy(bytes1[:, 1, :], x_byte_win[:].indirect(offs_sb[:]))
         nc.vector.tensor_copy(bytes1[:, 2, :], d_byte_win[:].indirect(k2_sb[:]))
+        nc.vector.tensor_copy(bytes1[:, 1, :], x_byte_win[:].indirect(offs_sb[:]))
         place_rows(planes1[:].rearrange("p l n -> p (l n)"), 0, bytes1[:].rearrange("p l n -> p (l n)"))
+
+        gs_sb = shared.tile([P, 1, PACK], F32, align_bytes=64, offset=12288)
+        nc.sync.dma_start(gs_sb[:, 0, :], gs.rearrange("(p t) o -> p (t o)", t=PACK))
 
         d1_words = keep.tile([P, H], U32, align_bytes=64)
         d2_words = keep.tile([P, H], U32, align_bytes=64)
@@ -86,17 +88,22 @@ def tile_picked_pqres2_relu_po_kernel(
             nc.vector.tensor_copy(half[:], x_word_win[:].indirect(offs_sb[:, 16 * h : 16 * (h + 1)]))
             xq.append(half)
 
-        bytes2 = shared.tile([P, 2, H], U8, align_bytes=64, offset=0)
-        words2 = shared.tile([P, 2, H], U32, align_bytes=64, offset=2048)
-        nc.vector.tensor_copy(bytes2[:, 0, :], d_byte_win[:].indirect(k3_sb[:]))
-        place_rows(planes2[:], 0, bytes2[:, 0, :])
-        nc.vector.tensor_copy(bytes2[:, 1, :], d_byte_win[:].indirect(k4_sb[:]))
-        place_rows(planes2[:], 4, bytes2[:, 1, :])
-        nc.vector.tensor_copy(words2[:, 0, :], d_word_win[:].indirect(k3_sb[:]))
-        nc.vector.tensor_copy(words2[:, 1, :], d_word_win[:].indirect(k4_sb[:]))
-        w2 = keep.tile([P, 2, PACK, P], U32, align_bytes=64)
+        d3_bytes = shared.tile([P, H], U8, align_bytes=64, offset=0)
+        d4_bytes = shared.tile([P, H], U8, align_bytes=64, offset=512)
+        nc.vector.tensor_copy(d3_bytes[:], d_byte_win[:].indirect(k3_sb[:]))
+        place_rows(planes2[:], 0, d3_bytes[:])
+        nc.vector.tensor_copy(d4_bytes[:], d_byte_win[:].indirect(k4_sb[:]))
+        place_rows(planes2[:], 4, d4_bytes[:])
+
+        def dealt_words(list_sb, offset, name):
+            picked = shared.tile([P, H], U32, align_bytes=64, offset=offset, name=name + "_picked")
+            nc.vector.tensor_copy(picked[:], d_word_win[:].indirect(list_sb[:]))
+            dealt = keep.tile([P, PACK, P], U32, align_bytes=64, name=name + "_dealt")
+            nc.vector.tensor_copy(dealt[:].bitcast(I32).rearrange("p t m -> p m t"), picked[:].bitcast(I32).rearrange("p (m t) -> p m t", t=PACK))
+            return dealt
+
+        d4_dealt = dealt_words(k4_sb, 2048, "d4")
         s2 = keep.tile([P, PACK, P], U8, align_bytes=64)
-        nc.vector.tensor_copy(w2[:].bitcast(I32).rearrange("p l t m -> p l m t"), words2[:].bitcast(I32).rearrange("p l (m t) -> p l m t", t=PACK))
         nc.vector.tensor_copy(s2[:].rearrange("p t m -> p m t"), planes2[:].rearrange("p (m t) -> p m t", t=PACK))
 
         def first_products(c):
@@ -133,28 +140,32 @@ def tile_picked_pqres2_relu_po_kernel(
         y_scales = keep.tile([P, S], U8, align_bytes=64)
 
         def hidden(c):
-            z = keep.tile([P, CH, PACK], BF16, align_bytes=64, name="z%d" % c)
+            z = shared.tile([P, CH, PACK], BF16, align_bytes=64, name="z%d" % c, offset=8192 + 1024 * (0, 1, 1, 2)[c])
             nc.vector.scalar_tensor_tensor(
                 z[:], pre[c][:].rearrange("p t n -> p n t"), 0.0, gs_sb[:].to_broadcast([P, CH, PACK]), ALU.max, ALU.mult
             )
             return z
 
-        def second_products(c, z):
+        def quantise_hidden(c, z):
             z_words = keep.tile([P, CH], U32, align_bytes=64, name="zw%d" % c)
             z_scales = keep.tile([P, CH], U8, align_bytes=64, name="zs%d" % c)
             nc.vector.quantize_mx(out=z_words[:].bitcast(FP8X4), scales=z_scales[:], in_=z[:].rearrange("p n t -> p (n t)"))
-            accs = []
-            for l in (1, 0):
-                acc = psum.tile([P, PACK, CH], F32, tag="acc", name="acc")
-                for t in range(PACK):
-                    nc.tensor.matmul_mx(
-                        out=acc[:, t, :], lhsT=w2[:, l, t, :].bitcast(FP8X4), lhsT_scale=s2[4 * l : P, t, :],
-                        rhs=z_words[:].bitcast(FP8X4), rhs_scale=z_scales[:], start=True, stop=True,
-                    )
-                accs.append(acc)
+            return z_words, z_scales
+
+        def second_product(dealt, first_row, z_words, z_scales):
+            acc = psum.tile([P, PACK, CH], F32, tag="acc", name="acc")
+            for t in range(PACK):
+                nc.tensor.matmul_mx(
+                    out=acc[:, t, :], lhsT=dealt[:, t, :].bitcast(FP8X4), lhsT_scale=s2[first_row:P, t, :],
+                    rhs=z_words[:].bitcast(FP8X4), rhs_scale=z_scales[:], start=True, stop=True,
+                )
+            return acc
+
+        def fine_part(c, zq):
+            acc = second_product(d4_dealt, 4, *zq)
             fine = keep.tile([P, PACK * CH], F32, align_bytes=64, name="fine%d" % c)
-            nc.scalar.activation(fine[:], accs[0][:].rearrange("p t n -> p (t n)"), ACT.Copy, scale=FINE)
-            return accs[1], fine
+            nc.scalar.activation(fine[:], acc[:].rearrange("p t n -> p (t n)"), ACT.Copy, scale=FINE)
+            return fine
 
         def combine(c, acc, fine):
             tok = slice(c * CH, (c + 1) * CH)
@@ -163,33 +174,44 @@ def tile_picked_pqres2_relu_po_kernel(
                 y[:].rearrange("p t n -> p (t n)"), acc[:].rearrange("p t n -> p (t n)"), COARSE, fine[:], ALU.mult, ALU.add
             )
             nc.sync.dma_start(y_view[:, :, tok], y[:])
-            y16 = keep.tile([P, CH, PACK], BF16, align_bytes=64, name="y16_%d" % c)
+            y16 = y16_pairs[c // 2][:, (c % 2) * CH : (c % 2 + 1) * CH, :]
             if c + 1 < NCH:
-                nc.scalar.copy(y16[:], y[:].rearrange("p t n -> p n t"))
+                nc.scalar.copy(y16, y[:].rearrange("p t n -> p n t"))
             else:
-                nc.vector.tensor_copy(y16[:], y[:].rearrange("p t n -> p n t"))
-            return y16
+                nc.vector.tensor_copy(y16, y[:].rearrange("p t n -> p n t"))
 
-        def hand_on(c, y16):
-            tok = slice(c * CH, (c + 1) * CH)
-            y_words = keep.tile([P, CH], U32, align_bytes=64, name="yw%d" % c)
-            nc.vector.quantize_mx(out=y_words[:].bitcast(FP8X4), scales=y_scales[:, tok], in_=y16[:].rearrange("p n t -> p (n t)"))
-            nc.sync.dma_start(word_view[:, tok], y_words[:].bitcast(I32))
+        y16_pairs = [keep.tile([P, 2 * CH, PACK], BF16, align_bytes=64, name="y16_%d" % h) for h in range(2)]
+        word_pairs = [keep.tile([P, 2 * CH], U32, align_bytes=64, name="yw%d" % h) for h in range(2)]
 
-        zs = {}
-        prods = {}
-        y16s = {}
-        for step in range(NCH + 3):
-            if step < NCH:
-                zs[step] = hidden(step)
-            if 0 <= step - 2 < NCH:
-                y16s[step - 2] = combine(step - 2, *prods[step - 2])
-            if 0 <= step - 3 < NCH:
-                hand_on(step - 3, y16s[step - 3])
-            if 0 <= step - 1 < NCH:
-                prods[step - 1] = second_products(step - 1, zs[step - 1])
+        def quantise_result(h, lo, hi):
+            nc.vector.quantize_mx(
+                out=word_pairs[h][:, lo:hi].bitcast(FP8X4),
+                scales=y_scales[:, 2 * CH * h + lo : 2 * CH * h + hi],
+                in_=y16_pairs[h][:, lo:hi, :].rearrange("p n t -> p (n t)"),
+            )
+
+        def store_words(h):
+            nc.sync.dma_start(word_view[:, 2 * CH * h : 2 * CH * (h + 1)], word_pairs[h][:].bitcast(I32))
+
+        zs = [hidden(0), hidden(1)]
+        zqs = [quantise_hidden(c, zs[c]) for c in range(2)]
+        fines = [fine_part(c, zqs[c]) for c in range(2)]
+        d3_dealt = dealt_words(k3_sb, 9216, "d3")
+        zs = zs + [hidden(2), hidden(3)]
+        zqs = zqs + [quantise_hidden(c, zs[c]) for c in range(2, 4)]
+        coarse = [second_product(d3_dealt, 0, *zqs[c]) for c in range(2)]
+        fines = fines + [fine_part(c, zqs[c]) for c in range(2, 4)]
+        coarse = coarse + [second_product(d3_dealt, 0, *zqs[c]) for c in range(2, 4)]
+        for c in range(NCH):
+            combine(c, coarse[c], fines[c])
+            if c == 2:
+                quantise_result(0, 0, 2 * CH)
+                store_words(0)
+        quantise_result(1, 0, CH)
+        quantise_result(1, CH, 2 * CH)
+        store_words(1)
 
         scale_view = out_2[0].bitcast(I32)
-        for a in range(4):
-            eng = nc.sync if a % 2 == 0 else nc.scalar
-            eng.dma_start(scale_view[a:16:4, :], y_scales[:].bitcast(I32)[a:P:32, :])
+        for q in range(4):
+            eng = nc.sync if q % 2 == 0 else nc.scalar
+            eng.dma_start(scale_view[4 * q : 4 * q + 4, :], y_scales[:].bitcast(I32)[32 * q : 32 * q + 4, :])

@@ -44,7 +44,7 @@ def tile_picked_pqres2_relu_po_kernel(
         d_word_win = keep.tile([P, G], U32, align_bytes=64)
         x_word_win = shared.tile([P, T], U32, align_bytes=64, offset=0)
         planes1 = keep.tile([P, 3, S], U8, align_bytes=64)
-        planes2 = shared.tile([P, H], U8, align_bytes=64, offset=10240)
+        planes2 = shared.tile([P, H], U8, align_bytes=64, offset=8192)
         ident = keep.tile([P, P], F32, align_bytes=64)
 
         nc.vector.memset(d_byte_win[:].bitcast(I32), 0)
@@ -95,14 +95,16 @@ def tile_picked_pqres2_relu_po_kernel(
         nc.vector.tensor_copy(d4_bytes[:], d_byte_win[:].indirect(k4_sb[:]))
         place_rows(planes2[:], 4, d4_bytes[:])
 
-        def dealt_words(list_sb, offset, name):
-            picked = shared.tile([P, H], U32, align_bytes=64, offset=offset, name=name + "_picked")
-            nc.vector.tensor_copy(picked[:], d_word_win[:].indirect(list_sb[:]))
-            dealt = keep.tile([P, PACK, P], U32, align_bytes=64, name=name + "_dealt")
-            nc.vector.tensor_copy(dealt[:].bitcast(I32).rearrange("p t m -> p m t"), picked[:].bitcast(I32).rearrange("p (m t) -> p m t", t=PACK))
-            return dealt
+        d4_words = shared.tile([P, H], U32, align_bytes=64, offset=2048)
+        d3_words = shared.tile([P, H], U32, align_bytes=64, offset=4096)
+        nc.vector.tensor_copy(d4_words[:], d_word_win[:].indirect(k4_sb[:]))
+        nc.vector.tensor_copy(d3_words[:], d_word_win[:].indirect(k3_sb[:]))
 
-        d4_dealt = dealt_words(k4_sb, 2048, "d4")
+        def deal_words(dealt, picked):
+            nc.vector.tensor_copy(dealt[:].bitcast(I32).rearrange("p t m -> p m t"), picked[:].bitcast(I32).rearrange("p (m t) -> p m t", t=PACK))
+
+        d4_dealt = keep.tile([P, PACK, P], U32, align_bytes=64)
+        deal_words(d4_dealt, d4_words)
         s2 = keep.tile([P, PACK, P], U8, align_bytes=64)
         nc.vector.tensor_copy(s2[:].rearrange("p t m -> p m t"), planes2[:].rearrange("p (m t) -> p m t", t=PACK))
 
@@ -140,7 +142,7 @@ def tile_picked_pqres2_relu_po_kernel(
         y_scales = keep.tile([P, S], U8, align_bytes=64)
 
         def hidden(c):
-            z = shared.tile([P, CH, PACK], BF16, align_bytes=64, name="z%d" % c, offset=8192 + 1024 * (0, 1, 1, 2)[c])
+            z = shared.tile([P, CH, PACK], BF16, align_bytes=64, name="z%d" % c, offset=(8192, 9216, 4096, 16384)[c])
             nc.vector.scalar_tensor_tensor(
                 z[:], pre[c][:].rearrange("p t n -> p n t"), 0.0, gs_sb[:].to_broadcast([P, CH, PACK]), ALU.max, ALU.mult
             )
@@ -163,7 +165,7 @@ def tile_picked_pqres2_relu_po_kernel(
 
         def fine_part(c, zq):
             acc = second_product(d4_dealt, 4, *zq)
-            fine = keep.tile([P, PACK * CH], F32, align_bytes=64, name="fine%d" % c)
+            fine = shared.tile([P, PACK * CH], F32, align_bytes=64, name="fine%d" % c, offset=16384 + 2048 * c)
             nc.scalar.activation(fine[:], acc[:].rearrange("p t n -> p (t n)"), ACT.Copy, scale=FINE)
             return fine
 
@@ -181,7 +183,6 @@ def tile_picked_pqres2_relu_po_kernel(
                 nc.vector.tensor_copy(y16, y[:].rearrange("p t n -> p n t"))
 
         y16_pairs = [keep.tile([P, 2 * CH, PACK], BF16, align_bytes=64, name="y16_%d" % h) for h in range(2)]
-        word_pairs = [keep.tile([P, 2 * CH], U32, align_bytes=64, name="yw%d" % h) for h in range(2)]
 
         def quantise_result(h, lo, hi):
             nc.vector.quantize_mx(
@@ -190,26 +191,27 @@ def tile_picked_pqres2_relu_po_kernel(
                 in_=y16_pairs[h][:, lo:hi, :].rearrange("p n t -> p (n t)"),
             )
 
-        def store_words(h):
-            nc.sync.dma_start(word_view[:, 2 * CH * h : 2 * CH * (h + 1)], word_pairs[h][:].bitcast(I32))
+        def store_words(eng, h):
+            eng.dma_start(word_view[:, 2 * CH * h : 2 * CH * (h + 1)], word_pairs[h][:].bitcast(I32))
 
         zs = [hidden(0), hidden(1)]
         zqs = [quantise_hidden(c, zs[c]) for c in range(2)]
         fines = [fine_part(c, zqs[c]) for c in range(2)]
-        d3_dealt = dealt_words(k3_sb, 9216, "d3")
-        zs = zs + [hidden(2), hidden(3)]
-        zqs = zqs + [quantise_hidden(c, zs[c]) for c in range(2, 4)]
+        d3_dealt = shared.tile([P, PACK, P], U32, align_bytes=64, offset=8192)
+        deal_words(d3_dealt, d3_words)
         coarse = [second_product(d3_dealt, 0, *zqs[c]) for c in range(2)]
-        fines = fines + [fine_part(c, zqs[c]) for c in range(2, 4)]
-        coarse = coarse + [second_product(d3_dealt, 0, *zqs[c]) for c in range(2, 4)]
-        for c in range(NCH):
+        for c in range(2, NCH):
+            zs.append(hidden(c))
+            combine(c - 2, coarse[c - 2], fines[c - 2])
+            zqs.append(quantise_hidden(c, zs[c]))
+            fines.append(fine_part(c, zqs[c]))
+            coarse.append(second_product(d3_dealt, 0, *zqs[c]))
+        for c in range(2, NCH):
             combine(c, coarse[c], fines[c])
-            if c == 2:
-                quantise_result(0, 0, 2 * CH)
-                store_words(0)
-        quantise_result(1, 0, CH)
-        quantise_result(1, CH, 2 * CH)
-        store_words(1)
+        word_pairs = [shared.tile([P, 2 * CH], U32, align_bytes=64, name="yw%d" % h, offset=16384 + 2048 * 3 + 1024 * h) for h in range(2)]
+        for h, eng in enumerate((nc.sync, nc.scalar)):
+            quantise_result(h, 0, 2 * CH)
+            store_words(eng, h)
 
         scale_view = out_2[0].bitcast(I32)
         for q in range(4):

@@ -142,14 +142,14 @@ def tile_picked_pqres2_relu_po_kernel(
         y_scales = keep.tile([P, S], U8, align_bytes=64)
 
         def hidden(c):
-            z = shared.tile([P, CH, PACK], BF16, align_bytes=64, name="z%d" % c, offset=(8192, 9216, 4096, 16384)[c])
+            z = shared.tile([P, CH, PACK], BF16, align_bytes=64, name="z%d" % c, offset=(8192, 9216, 4096, 5120)[c])
             nc.vector.scalar_tensor_tensor(
                 z[:], pre[c][:].rearrange("p t n -> p n t"), 0.0, gs_sb[:].to_broadcast([P, CH, PACK]), ALU.max, ALU.mult
             )
             return z
 
         def quantise_hidden(c, z):
-            z_words = keep.tile([P, CH], U32, align_bytes=64, name="zw%d" % c)
+            z_words = shared.tile([P, CH], U32, align_bytes=64, name="zw%d" % c, offset=(13312, 13824, 12288, 12800)[c])
             z_scales = keep.tile([P, CH], U8, align_bytes=64, name="zs%d" % c)
             nc.vector.quantize_mx(out=z_words[:].bitcast(FP8X4), scales=z_scales[:], in_=z[:].rearrange("p n t -> p (n t)"))
             return z_words, z_scales
@@ -176,19 +176,21 @@ def tile_picked_pqres2_relu_po_kernel(
                 y[:].rearrange("p t n -> p (t n)"), acc[:].rearrange("p t n -> p (t n)"), COARSE, fine[:], ALU.mult, ALU.add
             )
             nc.sync.dma_start(y_view[:, :, tok], y[:])
-            y16 = y16_pairs[c // 2][:, (c % 2) * CH : (c % 2 + 1) * CH, :]
+            y16 = y16s[c]
             if c + 1 < NCH:
                 nc.scalar.copy(y16, y[:].rearrange("p t n -> p n t"))
             else:
                 nc.vector.tensor_copy(y16, y[:].rearrange("p t n -> p n t"))
 
-        y16_pairs = [keep.tile([P, 2 * CH, PACK], BF16, align_bytes=64, name="y16_%d" % h) for h in range(2)]
+        y16_early = keep.tile([P, 2 * CH, PACK], BF16, align_bytes=64)
+        y16_late = [keep.tile([P, CH, PACK], BF16, align_bytes=64, name="y16_%d" % c) for c in range(2, NCH)]
+        y16s = [y16_early[:, 0:CH, :], y16_early[:, CH : 2 * CH, :], y16_late[0][:], y16_late[1][:]]
 
-        def quantise_result(h, lo, hi):
+        def quantise_result(h, lo, hi, y16):
             nc.vector.quantize_mx(
                 out=word_pairs[h][:, lo:hi].bitcast(FP8X4),
                 scales=y_scales[:, 2 * CH * h + lo : 2 * CH * h + hi],
-                in_=y16_pairs[h][:, lo:hi, :].rearrange("p n t -> p (n t)"),
+                in_=y16.rearrange("p n t -> p (n t)"),
             )
 
         def store_words(eng, h):
@@ -200,18 +202,18 @@ def tile_picked_pqres2_relu_po_kernel(
         d3_dealt = shared.tile([P, PACK, P], U32, align_bytes=64, offset=8192)
         deal_words(d3_dealt, d3_words)
         coarse = [second_product(d3_dealt, 0, *zqs[c]) for c in range(2)]
-        for c in range(2, NCH):
-            zs.append(hidden(c))
-            combine(c - 2, coarse[c - 2], fines[c - 2])
-            zqs.append(quantise_hidden(c, zs[c]))
-            fines.append(fine_part(c, zqs[c]))
-            coarse.append(second_product(d3_dealt, 0, *zqs[c]))
-        for c in range(2, NCH):
+        zs = zs + [hidden(c) for c in range(2, NCH)]
+        zqs = zqs + [quantise_hidden(c, zs[c]) for c in range(2, NCH)]
+        fines = fines + [fine_part(c, zqs[c]) for c in range(2, NCH)]
+        coarse = coarse + [second_product(d3_dealt, 0, *zqs[c]) for c in range(2, NCH)]
+        for c in range(NCH):
             combine(c, coarse[c], fines[c])
         word_pairs = [shared.tile([P, 2 * CH], U32, align_bytes=64, name="yw%d" % h, offset=16384 + 2048 * 3 + 1024 * h) for h in range(2)]
-        for h, eng in enumerate((nc.sync, nc.scalar)):
-            quantise_result(h, 0, 2 * CH)
-            store_words(eng, h)
+        quantise_result(0, 0, 2 * CH, y16_early[:])
+        store_words(nc.sync, 0)
+        quantise_result(1, 0, CH, y16s[2])
+        quantise_result(1, CH, 2 * CH, y16s[3])
+        store_words(nc.scalar, 1)
 
         scale_view = out_2[0].bitcast(I32)
         for q in range(4):

from contextlib import ExitStack

import concourse.mybir as mybir
from concourse.masks import make_identity

K, T, S, G, H = 512, 2048, 512, 2048, 512
FLOPS = 4 * 2 * K * H * S

F32 = mybir.dt.float32
BF16 = mybir.dt.bfloat16
I32 = mybir.dt.int32
U32 = mybir.dt.uint32
U16 = mybir.dt.uint16
U8 = mybir.dt.uint8
FP8X4 = mybir.dt.float8_e4m3fn_x4
ALU = mybir.AluOpType
ACT = mybir.ActivationFunctionType

P = 128
PACK = 4
CH = 128
NCH = S // CH
COARSE = 0.0625
FINE = 0.0625 * 0.25


def tile_picked_pqres2_relu_po_kernel(
    tc, x_words, x_scales, d_words, d_scales, gs, offs, k1, k2, k3, k4, out_0, out_1, out_2
):
    nc = tc.nc
    with ExitStack() as ctx:
        lists = ctx.enter_context(tc.tile_pool(name="lists", bufs=1))
        keep = ctx.enter_context(tc.tile_pool(name="keep", bufs=1))
        shared = ctx.enter_context(tc.tile_pool(name="shared", bufs=1))
        psum = ctx.enter_context(tc.psum_pool(name="psum", bufs=8))

        def list_tile(name):
            return lists.tile([P, S // 16], U16, name=name)

        k1_sb, k2_sb, k3_sb, k4_sb, offs_sb = [list_tile(n) for n in ("k1_sb", "k2_sb", "k3_sb", "k4_sb", "offs_sb")]

        d_byte_win = keep.tile([P, G], U8, align_bytes=64)
        x_byte_win = shared.tile([P, T], U8, align_bytes=64, offset=12288)
        d_word_win = keep.tile([P, G], U32, align_bytes=64)
        x_word_win = shared.tile([P, T], U32, align_bytes=64, offset=0)
        planes1 = keep.tile([P, 3, S], U8, align_bytes=64)
        planes2 = shared.tile([P, H], U8, align_bytes=64, offset=8192)
        ident = keep.tile([P, P], F32, align_bytes=64)

        nc.vector.memset(d_byte_win[:].bitcast(I32), 0)
        nc.vector.memset(x_byte_win[:].bitcast(I32), 0)

        nc.sync.dma_start(k1_sb[:], k1)
        nc.sync.dma_start(d_byte_win[:].bitcast(I32)[0:P:8, :], d_scales[0].bitcast(I32))
        nc.sync.dma_start(offs_sb[:], offs)
        nc.sync.dma_start(x_byte_win[:].bitcast(I32)[0:P:8, :], x_scales[0].bitcast(I32))
        nc.sync.dma_start(k2_sb[:], k2)
        nc.sync.dma_start(k3_sb[:], k3)
        nc.sync.dma_start(k4_sb[:], k4)
        nc.sync.dma_start(d_word_win[:].bitcast(I32), d_words[0].rearrange("p n t -> p (n t)").bitcast(I32))
        nc.sync.dma_start(x_word_win[:].bitcast(I32), x_words[0].rearrange("p n t -> p (n t)").bitcast(I32))

        nc.vector.memset(planes1[:].rearrange("p l n -> p (l n)").bitcast(I32), 0)
        nc.vector.memset(planes2[:].bitcast(I32), 0)
        make_identity(nc, ident[:])

        def place_rows(planes, first_row, picked):
            for q in range(4):
                row = 32 * q + first_row
                nc.sync.dma_start(planes.bitcast(I32)[row : row + 4, :], picked.bitcast(I32)[32 * q : 32 * q + 32 : 8, :])

        bytes1 = keep.tile([P, 3, S], U8, align_bytes=64)
        nc.vector.tensor_copy(bytes1[:, 0, :], d_byte_win[:].indirect(k1_sb[:]))
        nc.vector.tensor_copy(bytes1[:, 2, :], d_byte_win[:].indirect(k2_sb[:]))
        nc.vector.tensor_copy(bytes1[:, 1, :], x_byte_win[:].indirect(offs_sb[:]))
        place_rows(planes1[:].rearrange("p l n -> p (l n)"), 0, bytes1[:].rearrange("p l n -> p (l n)"))

        gs_sb = shared.tile([P, 1, PACK], F32, align_bytes=64, offset=12288)
        nc.sync.dma_start(gs_sb[:, 0, :], gs.rearrange("(p t) o -> p (t o)", t=PACK))

        d1_words = keep.tile([P, H], U32, align_bytes=64)
        d2_words = keep.tile([P, H], U32, align_bytes=64)
        nc.vector.tensor_copy(d1_words[:], d_word_win[:].indirect(k1_sb[:]))
        nc.vector.tensor_copy(d2_words[:], d_word_win[:].indirect(k2_sb[:]))
        xq = []
        for h in range(2):
            half = keep.tile([P, S // 2], U32, align_bytes=64, name="xq%d" % h)
            nc.vector.tensor_copy(half[:], x_word_win[:].indirect(offs_sb[:, 16 * h : 16 * (h + 1)]))
            xq.append(half)

        d3_bytes = shared.tile([P, H], U8, align_bytes=64, offset=0)
        d4_bytes = shared.tile([P, H], U8, align_bytes=64, offset=512)
        nc.vector.tensor_copy(d3_bytes[:], d_byte_win[:].indirect(k3_sb[:]))
        place_rows(planes2[:], 0, d3_bytes[:])
        nc.vector.tensor_copy(d4_bytes[:], d_byte_win[:].indirect(k4_sb[:]))
        place_rows(planes2[:], 4, d4_bytes[:])

        d4_words = shared.tile([P, H], U32, align_bytes=64, offset=2048)
        d3_words = shared.tile([P, H], U32, align_bytes=64, offset=4096)
        nc.vector.tensor_copy(d4_words[:], d_word_win[:].indirect(k4_sb[:]))
        nc.vector.tensor_copy(d3_words[:], d_word_win[:].indirect(k3_sb[:]))

        def deal_words(dealt, picked):
            nc.vector.tensor_copy(dealt[:].bitcast(I32).rearrange("p t m -> p m t"), picked[:].bitcast(I32).rearrange("p (m t) -> p m t", t=PACK))

        d4_dealt = keep.tile([P, PACK, P], U32, align_bytes=64)
        deal_words(d4_dealt, d4_words)
        s2 = keep.tile([P, PACK, P], U8, align_bytes=64)
        nc.vector.tensor_copy(s2[:].rearrange("p t m -> p m t"), planes2[:].rearrange("p (m t) -> p m t", t=PACK))

        def first_products(c):
            tok = slice(c * CH, (c + 1) * CH)
            x_c = xq[c // 2][:, (c % 2) * CH : (c % 2 + 1) * CH]
            parts = []
            for words, plane, factor in ((d1_words, 0, COARSE), (d2_words, 2, FINE)):
                acc = psum.tile([P, H], F32, tag="acc", name="acc")
                nc.tensor.matmul_mx(
                    out=acc[:], lhsT=x_c.bitcast(FP8X4), lhsT_scale=planes1[:, 1, tok],
                    rhs=words[:].bitcast(FP8X4), rhs_scale=planes1[:, plane, :], start=True, stop=True,
                )
                part = keep.tile([P, PACK, P], F32, align_bytes=64, name="part%d_%d" % (c, plane))
                nc.scalar.activation(part[:], acc[:].rearrange("p (m t) -> p t m", t=PACK), ACT.Copy, scale=factor)
                parts.append(part)
            return parts

        def turn_and_add(parts):
            u = psum.tile([P, PACK, CH], F32, tag="acc", name="u")
            for t in range(PACK):
                for i, part in enumerate(parts):
                    nc.tensor.matmul(u[:, t, :], lhsT=part[:, t, :], rhs=ident[:], is_transpose=True, start=(i == 0), stop=(i == 1))
            return u

        pre = []
        parts = first_products(0)
        for c in range(NCH):
            nxt = first_products(c + 1) if c + 1 < NCH else None
            pre.append(turn_and_add(parts))
            parts = nxt

        y_view = out_0.rearrange("(p t) n -> p t n", t=PACK)
        word_view = out_1[0].rearrange("p n t -> p (n t)").bitcast(I32)
        y_scales = keep.tile([P, S], U8, align_bytes=64)

        def hidden(c):
            z = shared.tile([P, CH, PACK], BF16, align_bytes=64, name="z%d" % c, offset=(8192, 9216, 4096, 5120)[c])
            nc.vector.scalar_tensor_tensor(
                z[:], pre[c][:].rearrange("p t n -> p n t"), 0.0, gs_sb[:].to_broadcast([P, CH, PACK]), ALU.max, ALU.mult
            )
            return z

        def quantise_hidden(c, z):
            z_words = shared.tile([P, CH], U32, align_bytes=64, name="zw%d" % c, offset=(13312, 13824, 12288, 12800)[c])
            z_scales = keep.tile([P, CH], U8, align_bytes=64, name="zs%d" % c)
            nc.vector.quantize_mx(out=z_words[:].bitcast(FP8X4), scales=z_scales[:], in_=z[:].rearrange("p n t -> p (n t)"))
            return z_words, z_scales

        def second_product(dealt, first_row, z_words, z_scales):
            acc = psum.tile([P, PACK, CH], F32, tag="acc", name="acc")
            for t in range(PACK):
                nc.tensor.matmul_mx(
                    out=acc[:, t, :], lhsT=dealt[:, t, :].bitcast(FP8X4), lhsT_scale=s2[first_row:P, t, :],
                    rhs=z_words[:].bitcast(FP8X4), rhs_scale=z_scales[:], start=True, stop=True,
                )
            return acc

        def fine_part(c, zq):
            acc = second_product(d4_dealt, 4, *zq)
            fine = shared.tile([P, PACK * CH], F32, align_bytes=64, name="fine%d" % c, offset=16384 + 2048 * c)
            nc.scalar.activation(fine[:], acc[:].rearrange("p t n -> p (t n)"), ACT.Copy, scale=FINE)
            return fine

        def combine(c, acc, fine):
            tok = slice(c * CH, (c + 1) * CH)
            y = keep.tile([P, PACK, CH], F32, align_bytes=64, name="y%d" % c)
            nc.vector.scalar_tensor_tensor(
                y[:].rearrange("p t n -> p (t n)"), acc[:].rearrange("p t n -> p (t n)"), COARSE, fine[:], ALU.mult, ALU.add
            )
            nc.sync.dma_start(y_view[:, :, tok], y[:])
            y16 = y16s[c]
            if c + 1 < NCH:
                nc.scalar.copy(y16, y[:].rearrange("p t n -> p n t"))
            else:
                nc.vector.tensor_copy(y16, y[:].rearrange("p t n -> p n t"))

        y16_early = keep.tile([P, 2 * CH, PACK], BF16, align_bytes=64)
        y16_late = [keep.tile([P, CH, PACK], BF16, align_bytes=64, name="y16_%d" % c) for c in range(2, NCH)]
        y16s = [y16_early[:, 0:CH, :], y16_early[:, CH : 2 * CH, :], y16_late[0][:], y16_late[1][:]]

        def quantise_result(h, lo, hi, y16):
            nc.vector.quantize_mx(
                out=word_pairs[h][:, lo:hi].bitcast(FP8X4),
                scales=y_scales[:, 2 * CH * h + lo : 2 * CH * h + hi],
                in_=y16.rearrange("p n t -> p (n t)"),
            )

        def store_words(eng, h):
            eng.dma_start(word_view[:, 2 * CH * h : 2 * CH * (h + 1)], word_pairs[h][:].bitcast(I32))

        zs = [hidden(0), hidden(1)]
        zqs = [quantise_hidden(c, zs[c]) for c in range(2)]
        fines = [fine_part(c, zqs[c]) for c in range(2)]
        d3_dealt = shared.tile([P, PACK, P], U32, align_bytes=64, offset=8192)
        deal_words(d3_dealt, d3_words)
        coarse = [second_product(d3_dealt, 0, *zqs[c]) for c in range(2)]
        zs = zs + [hidden(c) for c in range(2, NCH)]
        zqs = zqs + [quantise_hidden(c, zs[c]) for c in range(2, NCH)]
        fines = fines + [fine_part(c, zqs[c]) for c in range(2, NCH)]
        coarse = coarse + [second_product(d3_dealt, 0, *zqs[c]) for c in range(2, NCH)]
        for c in range(NCH):
            combine(c, coarse[c], fines[c])
        word_pairs = [shared.tile([P, 2 * CH], U32, align_bytes=64, name="yw%d" % h, offset=16384 + 2048 * 3 + 1024 * h) for h in range(2)]
        quantise_result(0, 0, 2 * CH, y16_early[:])
        store_words(nc.sync, 0)
        quantise_result(1, 0, CH, y16s[2])
        quantise_result(1, CH, 2 * CH, y16s[3])
        store_words(nc.scalar, 1)

        scale_view = out_2[0].bitcast(I32)
        for q in range(4):
            eng = nc.sync if q % 2 == 0 else nc.scalar
            eng.dma_start(scale_view[4 * q : 4 * q + 4, :], y_scales[:].bitcast(I32)[32 * q : 32 * q + 4, :])
